import numpy as np
import ml_dtypes


def mxq(x, axis, fmt="e4m3"):
    dtype, down = {"e4m3": (ml_dtypes.float8_e4m3fn, 7), "e5m2": (ml_dtypes.float8_e5m2, 14)}[fmt]
    v = np.moveaxis(np.asarray(x, np.float32).astype(ml_dtypes.bfloat16).astype(np.float64), axis, -1)
    blocks = v.reshape(v.shape[:-1] + (-1, 32))
    amax = np.abs(blocks).max(-1, keepdims=True)
    byte = np.maximum(np.where(amax > 0, np.frexp(amax)[1] - 1 + 127, 0) - down, 1)
    scale = np.exp2(byte - 127.0)
    codes = (blocks / scale).astype(np.float32).astype(dtype).astype(np.float64)
    return np.moveaxis((codes * scale).reshape(v.shape), -1, axis)


WIDE = False


def mx_kscale(k):
    if not WIDE:
        return np.ones(k)
    levels = np.array([10, -10, 5, -5, 0])
    if k % 512:
        return np.exp2(np.random.permutation(np.resize(levels, k // 32))).repeat(32)
    a = np.empty((k // 512, 16))
    for p in range(k // 512):
        a[p, :8] = np.random.permutation(np.resize(levels, 8))
        for g in range(8):
            far = levels[np.abs(levels - a[p, g]) >= 10]
            a[p, g + 8] = far[np.random.randint(len(far))]
    return np.exp2(a.ravel()).repeat(32)


def f64(x):
    return np.asarray(x).astype(np.float64)


def striped(idx):
    return np.tile(np.asarray(idx).reshape(-1, 16).T, (8, 1)).astype(np.uint16)


def unstriped(offs):
    return offs[:16].T.reshape(-1).astype(np.int64)


E2M1 = np.array([0.0, 0.5, 1.0, 1.5, 2.0, 3.0, 4.0, 6.0, -0.0, -0.5, -1.0, -1.5, -2.0, -3.0, -4.0, -6.0])


def pack_weight(w, fmt):
    k, n = w.shape
    w = f64(np.asarray(w, np.float32).astype(ml_dtypes.bfloat16)).reshape(k // 32, 32, n)
    amax = np.abs(w).max(1)
    if fmt == "e4m3":
        byte = np.frexp(amax)[1] - 1 + 127 - 7
    else:
        mant, ex = np.frexp(amax / 6.0)
        byte = np.where(mant > 0.5, ex, ex - 1) + 127
    byte = np.clip(np.where(amax > 0, byte, 1), 1, 254)
    scaled = (w * np.exp2(127.0 - byte)[:, None, :]).reshape(k, n).astype(np.float32)
    by_word = np.ascontiguousarray(scaled.reshape(k // 512, 128, 4, n).transpose(0, 1, 3, 2))
    if fmt == "e4m3":
        words = by_word.astype(ml_dtypes.float8_e4m3fn).view(np.uint8)
    else:
        c = by_word.astype(ml_dtypes.float4_e2m1fn).view(np.uint8) & 0xF
        words = (c[..., 0::2] | (c[..., 1::2] << 4)).reshape(k // 512, 128, 2 * n)
    return np.ascontiguousarray(words), np.ascontiguousarray(byte.astype(np.uint8).reshape(k // 512, 16, n))


def unpack_weight(words, scales, fmt):
    g, _, n = scales.shape
    words = np.ascontiguousarray(words).reshape(g, 128, n, -1)
    if fmt == "e4m3":
        vals = words.view(ml_dtypes.float8_e4m3fn).astype(np.float64)
    else:
        nib = np.empty((g, 128, n, 4), np.uint8)
        nib[..., 0::2] = words & 0xF
        nib[..., 1::2] = words >> 4
        vals = E2M1[nib]
    vals = vals * np.repeat(np.exp2(scales.astype(np.float64) - 127.0), 8, axis=1)[..., None]
    return vals.transpose(0, 1, 3, 2).reshape(g * 512, n)


def sigmoid(v):
    return 1.0 / (1.0 + np.exp(-v))


def bf(x):
    return np.asarray(x, np.float32).astype(ml_dtypes.bfloat16)


def planes(Y):
    r, m = Y.shape
    b = f64(bf(Y)).reshape(r // 32, 32, m)
    amax = np.abs(b).max(1)
    byte = np.clip(np.where(amax > 0, np.frexp(amax)[1] - 1 + 127 - 7, 1), 1, 254)
    codes = (b * np.exp2(127.0 - byte)[:, None, :]).reshape(r, m).astype(np.float32).astype(ml_dtypes.float8_e4m3fn).view(np.uint8)
    words = codes.reshape(r // 512, 128, 4, m).transpose(0, 1, 3, 2)
    return np.ascontiguousarray(words), np.ascontiguousarray(byte.astype(np.uint8).reshape(r // 512, 16, m))


B, N, T, D, NQ = 1, 512, 2048, 1024, 512


def setup_inputs():
    n = np.random.standard_normal
    idx = np.random.permutation(T)[:B * N]
    s = mx_kscale(D)[:, None]
    kp = pack_weight(n((D, T)) / s, "e2m1")
    cp = pack_weight(n((D, T)) / s, "e4m3")
    return {
        "qT": (n((B, D, NQ)) * s * (1.00 / np.sqrt(D))).astype(np.float32),
        "k_words": np.ascontiguousarray(kp[0].reshape(1, 2, 128, T, 2).transpose(0, 2, 3, 1, 4)).reshape(1, 128, T, 4),
        "k_scales": kp[1],
        "c_words": cp[0],
        "c_scales": cp[1],
        "offs": striped(idx),
    }


def reference(qT, k_words, k_scales, c_words, c_scales, offs):
    idx = unstriped(offs)
    pick = lambda x, which: x[:, which].reshape(x.shape[0], B, -1).transpose(1, 0, 2)
    k = unpack_weight(k_words.reshape(1, 128, T, 2, 2).transpose(0, 3, 1, 2, 4).reshape(2, 128, 2 * T), k_scales, "e2m1")
    kg = pick(k, idx)
    c = unpack_weight(c_words, c_scales, "e4m3")
    cg = pick(c, idx)
    qq = mxq(f64(qT), 1, "e4m3")
    a = kg.transpose(0, 2, 1) @ qq
    z = cg.transpose(0, 2, 1) @ qq
    y = sigmoid(a) * z
    Y = y[0]
    words, scales = planes(Y)
    return Y, words, scales

@@ -1,0 +1,178 @@
+from contextlib import ExitStack
+
+import concourse.mybir as mybir
+
+D, T, SLOTS, NQ = 1024, 2048, 512, 512
+FLOPS = 2 * 2 * SLOTS * NQ * D
+
+F32 = mybir.dt.float32
+BF16 = mybir.dt.bfloat16
+I32 = mybir.dt.int32
+U32 = mybir.dt.uint32
+U16 = mybir.dt.uint16
+U8 = mybir.dt.uint8
+FP8X4 = mybir.dt.float8_e4m3fn_x4
+FP4X4 = mybir.dt.float4_e2m1fn_x4
+
+P = 128
+PACK = 4
+K_PASS = P * PACK
+PASSES = D // K_PASS
+QUADRANTS = 4
+CHUNK = 128
+CHUNKS = NQ // CHUNK
+
+
+def dealt(ap):
+    return ap.rearrange("p (r s) -> p s r", r=PACK)
+
+
+def tile_attend_plh_mixglu_topk_kernel(tc, qT, k_words, k_scales, c_words, c_scales, offs, out_0, out_1, out_2):
+    nc = tc.nc
+    with ExitStack() as ctx:
+        pool = ctx.enter_context(tc.tile_pool(name="held", bufs=1))
+        psum = ctx.enter_context(tc.psum_pool(name="psum", bufs=1))
+
+        offsets = pool.tile([P, SLOTS // 16], U16, name="offsets")
+        q_raw = [pool.tile([P, PACK, NQ], F32, name=f"q_raw{g}", tag=f"stage{g + 1}") for g in range(PASSES)]
+        kw_all = pool.tile([P, T], U32, name="kw_all", tag="stage0")
+        ks_all = pool.tile([P, PASSES * T], U8, name="ks_all")
+        cs_all = pool.tile([P, T], U8, name="cs_all")
+
+        def load_q(g):
+            rows = qT[0, g * K_PASS : (g + 1) * K_PASS, :]
+            nc.sync.dma_start(out=q_raw[g][:], in_=rows.rearrange("(p j) n -> p j n", j=PACK))
+
+        def load_words(tile, words):
+            nc.sync.dma_start(out=tile[:].bitcast(I32), in_=words.rearrange("p t b -> p (t b)").bitcast(I32))
+
+        nc.vector.memset(ks_all[:].bitcast(I32), 0)
+        nc.gpsimd.memset(cs_all[:].bitcast(I32), 0)
+
+        nc.sync.dma_start(offsets[:], offs)
+        load_words(kw_all, k_words[0])
+        load_q(0)
+        load_q(1)
+        for Q in range(QUADRANTS):
+            nc.scalar.dma_start(
+                out=ks_all[32 * Q : 32 * Q + 4, :].bitcast(I32).rearrange("f (g t) -> f g t", g=PASSES),
+                in_=k_scales[:, 4 * Q : 4 * Q + 4, :].bitcast(I32).rearrange("g f t -> f g t"),
+            )
+        for Q in range(QUADRANTS):
+            nc.gpsimd.dma_start(
+                out=cs_all[32 * Q + 4 : 32 * Q + 12, :].bitcast(I32),
+                in_=c_scales[:, 4 * Q : 4 * Q + 4, :].bitcast(I32),
+            )
+
+        q_bf = [pool.tile([P, NQ, PACK], BF16, name=f"q_bf{g}", align_bytes=64) for g in range(PASSES)]
+        q_codes = [pool.tile([P, NQ], U32, name=f"q_codes{g}", align_bytes=64) for g in range(PASSES)]
+        q_scales = [pool.tile([P, NQ], U8, name=f"q_scales{g}", align_bytes=64) for g in range(PASSES)]
+
+        def interleave(dst, src):
+            nc.scalar.copy(
+                out=dst.rearrange("p (c i) t -> p c t i", i=4),
+                in_=src.rearrange("p t (c i) -> p c t i", i=4),
+            )
+
+        def quantize_q(g):
+            nc.vector.quantize_mx(
+                out=q_codes[g][:].bitcast(FP8X4),
+                scales=q_scales[g][:],
+                in_=q_bf[g][:].rearrange("p n t -> p (n t)"),
+            )
+
+        kw_listed = pool.tile([P, SLOTS], U32, name="kw_listed")
+        kw = pool.tile([P, PASSES * SLOTS * 2], U8, name="kw", align_bytes=64)
+        nc.vector.tensor_copy(kw_listed[:], kw_all[:].indirect(offsets[:]))
+        interleave(q_bf[0][:], q_raw[0][:])
+        cw_all = [pool.tile([P, T], U32, name=f"cw_all{g}", tag=f"stage{g}") for g in range(PASSES)]
+        load_words(cw_all[0], c_words[0])
+        load_words(cw_all[1], c_words[1])
+
+        ks_listed = pool.tile([P, PASSES * SLOTS], U8, name="ks_listed", tag="listed_scales", align_bytes=64)
+        ks = pool.tile([P, PASSES * SLOTS], U8, name="ks", align_bytes=64)
+        for g in range(PASSES):
+            nc.vector.tensor_copy(
+                ks_listed[:, g * SLOTS : (g + 1) * SLOTS], ks_all[:, g * T : (g + 1) * T].indirect(offsets[:])
+            )
+        nc.vector.tensor_copy(
+            out=kw[:].bitcast(U16).rearrange("p (g r c i) -> p g c r i", g=PASSES, r=PACK, i=4),
+            in_=kw_listed[:].bitcast(U16).rearrange("p (c i r g) -> p g c r i", g=PASSES, r=PACK, i=4),
+        )
+        nc.vector.tensor_copy(
+            out=ks[:].rearrange("p (g r c i) -> p g c r i", g=PASSES, r=PACK, i=16),
+            in_=ks_listed[:].rearrange("p (g c i r) -> p g c r i", g=PASSES, r=PACK, i=16),
+        )
+        quantize_q(0)
+
+        gate = [psum.tile([P, NQ], F32, name=f"gate{r}") for r in range(PACK)]
+
+        def gate_pass(g):
+            for r in range(PACK):
+                first = g * SLOTS + r * P
+                nc.tensor.matmul_mx(
+                    out=gate[r][:],
+                    lhsT=kw[:, 2 * first : 2 * (first + P)].bitcast(FP4X4),
+                    lhsT_scale=ks[:, first : first + P],
+                    rhs=q_codes[g][:].bitcast(FP8X4),
+                    rhs_scale=q_scales[g][:],
+                    start=(g == 0),
+                    stop=(g == PASSES - 1),
+                )
+
+        gate_pass(0)
+        interleave(q_bf[1][:], q_raw[1][:])
+        cs = pool.tile([P, SLOTS], U8, name="cs", tag="listed_scales", align_bytes=64)
+        nc.vector.tensor_copy(dealt(cs[:]), cs_all[:].indirect(offsets[:]))
+        quantize_q(1)
+        gate_pass(1)
+
+        sig = pool.tile([P, PACK, NQ], F32, name="sig")
+        for r in range(PACK):
+            nc.scalar.activation(sig[:, r, :], gate[r][:], mybir.ActivationFunctionType.Sigmoid)
+
+        layer = [psum.tile([P, PACK, CHUNK], F32, name=f"layer{j}") for j in range(CHUNKS)]
+        cw = [pool.tile([P, SLOTS], U32, name=f"cw{g}", align_bytes=64) for g in range(PASSES)]
+        for g in range(PASSES):
+            nc.vector.tensor_copy(dealt(cw[g][:]), cw_all[g][:].indirect(offsets[:]))
+            for j in range(CHUNKS):
+                cols = slice(j * CHUNK, (j + 1) * CHUNK)
+                for r in range(PACK):
+                    slots = slice(r * P, (r + 1) * P)
+                    nc.tensor.matmul_mx(
+                        out=layer[j][:, r, :],
+                        lhsT=cw[g][:, slots].bitcast(FP8X4),
+                        lhsT_scale=cs[4 * (g + 1) :, slots],
+                        rhs=q_codes[g][:, cols].bitcast(FP8X4),
+                        rhs_scale=q_scales[g][:, cols],
+                        start=(g == 0 and r == 0),
+                        stop=(g == PASSES - 1 and r == PACK - 1),
+                    )
+
+        y_codes = pool.tile([P, NQ], U32, name="y_codes", align_bytes=64)
+        y_scales = pool.tile([P, NQ], U8, name="y_scales", align_bytes=64)
+        y_rows = out_0.rearrange("(p r) n -> p r n", r=PACK)
+        code_rows = out_1[0].rearrange("p n u -> p (n u)").bitcast(I32)
+        y = [pool.tile([P, PACK, CHUNK], F32, name=f"y{j}") for j in range(CHUNKS)]
+        y_bf = [pool.tile([P, CHUNK, PACK], BF16, name=f"y_bf{j}", align_bytes=64) for j in range(CHUNKS)]
+        for j in range(CHUNKS):
+            cols = slice(j * CHUNK, (j + 1) * CHUNK)
+            nc.vector.tensor_tensor(y[j][:], layer[j][:], sig[:, :, cols], mybir.AluOpType.mult)
+            nc.sync.dma_start(out=y_rows[:, :, cols], in_=y[j][:])
+            interleave(y_bf[j][:], y[j][:])
+        for j in range(CHUNKS):
+            cols = slice(j * CHUNK, (j + 1) * CHUNK)
+            nc.vector.quantize_mx(
+                out=y_codes[:, cols].bitcast(FP8X4),
+                scales=y_scales[:, cols],
+                in_=y_bf[j][:].rearrange("p n t -> p (n t)"),
+            )
+            if j % 2 == 1:
+                half = slice((j - 1) * CHUNK, (j + 1) * CHUNK)
+                nc.sync.dma_start(out=code_rows[:, half], in_=y_codes[:, half].bitcast(I32))
+        for Q in range(QUADRANTS):
+            queue = nc.scalar if Q % 2 == 0 else nc.sync
+            queue.dma_start(
+                out=out_2[0, 4 * Q : 4 * Q + 4, :].bitcast(I32),
+                in_=y_scales[32 * Q : 32 * Q + 4, :].bitcast(I32),
+            )

@@ -23,10 +23,6 @@ CHUNK = 128
 CHUNKS = NQ // CHUNK
 
 
-def dealt(ap):
-    return ap.rearrange("p (r s) -> p s r", r=PACK)
-
-
 def tile_attend_plh_mixglu_topk_kernel(tc, qT, k_words, k_scales, c_words, c_scales, offs, out_0, out_1, out_2):
     nc = tc.nc
     with ExitStack() as ctx:
@@ -34,8 +30,8 @@ def tile_attend_plh_mixglu_topk_kernel(tc, qT, k_words, k_scales, c_words, c_sca
         psum = ctx.enter_context(tc.psum_pool(name="psum", bufs=1))
 
         offsets = pool.tile([P, SLOTS // 16], U16, name="offsets")
-        q_raw = [pool.tile([P, PACK, NQ], F32, name=f"q_raw{g}", tag=f"stage{g + 1}") for g in range(PASSES)]
-        kw_all = pool.tile([P, T], U32, name="kw_all", tag="stage0")
+        q_raw = [pool.tile([P, PACK, NQ], F32, name=f"q_raw{g}") for g in range(PASSES)]
+        kw_all = pool.tile([P, T], U32, name="kw_all", tag="window")
         ks_all = pool.tile([P, PASSES * T], U8, name="ks_all")
         cs_all = pool.tile([P, T], U8, name="cs_all")
 
@@ -53,6 +49,8 @@ def tile_attend_plh_mixglu_topk_kernel(tc, qT, k_words, k_scales, c_words, c_sca
         load_words(kw_all, k_words[0])
         load_q(0)
         load_q(1)
+        cw_all = [pool.tile([P, T], U32, name="cw_all0")]
+        load_words(cw_all[0], c_words[0])
         for Q in range(QUADRANTS):
             nc.scalar.dma_start(
                 out=ks_all[32 * Q : 32 * Q + 4, :].bitcast(I32).rearrange("f (g t) -> f g t", g=PASSES),
@@ -64,7 +62,7 @@ def tile_attend_plh_mixglu_topk_kernel(tc, qT, k_words, k_scales, c_words, c_sca
                 in_=c_scales[:, 4 * Q : 4 * Q + 4, :].bitcast(I32),
             )
 
-        q_bf = [pool.tile([P, NQ, PACK], BF16, name=f"q_bf{g}", align_bytes=64) for g in range(PASSES)]
+        q_bf = [pool.tile([P, NQ, PACK], BF16, name=f"q_bf{g}", tag=f"scratch{g}", align_bytes=64) for g in range(PASSES)]
         q_codes = [pool.tile([P, NQ], U32, name=f"q_codes{g}", align_bytes=64) for g in range(PASSES)]
         q_scales = [pool.tile([P, NQ], U8, name=f"q_scales{g}", align_bytes=64) for g in range(PASSES)]
 
@@ -85,11 +83,10 @@ def tile_attend_plh_mixglu_topk_kernel(tc, qT, k_words, k_scales, c_words, c_sca
         kw = pool.tile([P, PASSES * SLOTS * 2], U8, name="kw", align_bytes=64)
         nc.vector.tensor_copy(kw_listed[:], kw_all[:].indirect(offsets[:]))
         interleave(q_bf[0][:], q_raw[0][:])
-        cw_all = [pool.tile([P, T], U32, name=f"cw_all{g}", tag=f"stage{g}") for g in range(PASSES)]
-        load_words(cw_all[0], c_words[0])
+        cw_all.append(pool.tile([P, T], U32, name="cw_all1", tag="window"))
         load_words(cw_all[1], c_words[1])
 
-        ks_listed = pool.tile([P, PASSES * SLOTS], U8, name="ks_listed", tag="listed_scales", align_bytes=64)
+        ks_listed = pool.tile([P, PASSES * SLOTS], U8, name="ks_listed")
         ks = pool.tile([P, PASSES * SLOTS], U8, name="ks", align_bytes=64)
         for g in range(PASSES):
             nc.vector.tensor_copy(
@@ -122,8 +119,13 @@ def tile_attend_plh_mixglu_topk_kernel(tc, qT, k_words, k_scales, c_words, c_sca
 
         gate_pass(0)
         interleave(q_bf[1][:], q_raw[1][:])
-        cs = pool.tile([P, SLOTS], U8, name="cs", tag="listed_scales", align_bytes=64)
-        nc.vector.tensor_copy(dealt(cs[:]), cs_all[:].indirect(offsets[:]))
+        cs_listed = pool.tile([P, SLOTS], U8, name="cs_listed", tag="scratch0", align_bytes=64)
+        cs = pool.tile([P, SLOTS], U8, name="cs", align_bytes=64)
+        nc.vector.tensor_copy(cs_listed[:], cs_all[:].indirect(offsets[:]))
+        nc.vector.tensor_copy(
+            out=cs[:].rearrange("p (r c i) -> p c r i", r=PACK, i=16),
+            in_=cs_listed[:].rearrange("p (c i r) -> p c r i", r=PACK, i=16),
+        )
         quantize_q(1)
         gate_pass(1)
 
@@ -134,7 +136,12 @@ def tile_attend_plh_mixglu_topk_kernel(tc, qT, k_words, k_scales, c_words, c_sca
         layer = [psum.tile([P, PACK, CHUNK], F32, name=f"layer{j}") for j in range(CHUNKS)]
         cw = [pool.tile([P, SLOTS], U32, name=f"cw{g}", align_bytes=64) for g in range(PASSES)]
         for g in range(PASSES):
-            nc.vector.tensor_copy(dealt(cw[g][:]), cw_all[g][:].indirect(offsets[:]))
+            cw_listed = pool.tile([P, SLOTS], U32, name=f"cw_listed{g}", tag="scratch1", align_bytes=64)
+            nc.vector.tensor_copy(cw_listed[:], cw_all[g][:].indirect(offsets[:]))
+            nc.vector.tensor_copy(
+                out=cw[g][:].bitcast(I32).rearrange("p (r c i) -> p c r i", r=PACK, i=4),
+                in_=cw_listed[:].bitcast(I32).rearrange("p (c i r) -> p c r i", r=PACK, i=4),
+            )
             for j in range(CHUNKS):
                 cols = slice(j * CHUNK, (j + 1) * CHUNK)
                 for r in range(PACK):
@@ -154,24 +161,21 @@ def tile_attend_plh_mixglu_topk_kernel(tc, qT, k_words, k_scales, c_words, c_sca
         y_rows = out_0.rearrange("(p r) n -> p r n", r=PACK)
         code_rows = out_1[0].rearrange("p n u -> p (n u)").bitcast(I32)
         y = [pool.tile([P, PACK, CHUNK], F32, name=f"y{j}") for j in range(CHUNKS)]
-        y_bf = [pool.tile([P, CHUNK, PACK], BF16, name=f"y_bf{j}", align_bytes=64) for j in range(CHUNKS)]
+        y_bf = pool.tile([P, NQ, PACK], BF16, name="y_bf", align_bytes=64)
         for j in range(CHUNKS):
             cols = slice(j * CHUNK, (j + 1) * CHUNK)
             nc.vector.tensor_tensor(y[j][:], layer[j][:], sig[:, :, cols], mybir.AluOpType.mult)
             nc.sync.dma_start(out=y_rows[:, :, cols], in_=y[j][:])
-            interleave(y_bf[j][:], y[j][:])
-        for j in range(CHUNKS):
-            cols = slice(j * CHUNK, (j + 1) * CHUNK)
+            interleave(y_bf[:, cols, :], y[j][:])
+        for cols in (slice(0, NQ - CHUNK), slice(NQ - CHUNK, NQ)):
             nc.vector.quantize_mx(
                 out=y_codes[:, cols].bitcast(FP8X4),
                 scales=y_scales[:, cols],
-                in_=y_bf[j][:].rearrange("p n t -> p (n t)"),
+                in_=y_bf[:, cols, :].rearrange("p n t -> p (n t)"),
             )
-            if j % 2 == 1:
-                half = slice((j - 1) * CHUNK, (j + 1) * CHUNK)
-                nc.sync.dma_start(out=code_rows[:, half], in_=y_codes[:, half].bitcast(I32))
+            nc.scalar.dma_start(out=code_rows[:, cols], in_=y_codes[:, cols].bitcast(I32))
         for Q in range(QUADRANTS):
-            queue = nc.scalar if Q % 2 == 0 else nc.sync
+            queue = nc.sync if Q % 2 == 0 else nc.scalar
             queue.dma_start(
                 out=out_2[0, 4 * Q : 4 * Q + 4, :].bitcast(I32),
                 in_=y_scales[32 * Q : 32 * Q + 4, :].bitcast(I32),

@@ -21,6 +21,11 @@ PASSES = D // K_PASS
 QUADRANTS = 4
 CHUNK = 128
 CHUNKS = NQ // CHUNK
+SPLIT = 320
+
+
+def dealt(ap):
+    return ap.rearrange("p (r s) -> p s r", r=PACK)
 
 
 def tile_attend_plh_mixglu_topk_kernel(tc, qT, k_words, k_scales, c_words, c_scales, offs, out_0, out_1, out_2):
@@ -31,8 +36,8 @@ def tile_attend_plh_mixglu_topk_kernel(tc, qT, k_words, k_scales, c_words, c_sca
 
         offsets = pool.tile([P, SLOTS // 16], U16, name="offsets")
         q_raw = [pool.tile([P, PACK, NQ], F32, name=f"q_raw{g}") for g in range(PASSES)]
-        kw_all = pool.tile([P, T], U32, name="kw_all", tag="window")
-        ks_all = pool.tile([P, PASSES * T], U8, name="ks_all")
+        kw_all = pool.tile([P, T], U32, name="kw_all")
+        ks_all = pool.tile([P, T], U8, name="ks_all", tag="window")
         cs_all = pool.tile([P, T], U8, name="cs_all")
 
         def load_q(g):
@@ -40,34 +45,37 @@ def tile_attend_plh_mixglu_topk_kernel(tc, qT, k_words, k_scales, c_words, c_sca
             nc.sync.dma_start(out=q_raw[g][:], in_=rows.rearrange("(p j) n -> p j n", j=PACK))
 
         def load_words(tile, words):
-            nc.sync.dma_start(out=tile[:].bitcast(I32), in_=words.rearrange("p t b -> p (t b)").bitcast(I32))
+            nc.sync.dma_start(out=tile.bitcast(I32), in_=words.rearrange("p t b -> p (t b)").bitcast(I32))
 
-        nc.vector.memset(ks_all[:].bitcast(I32), 0)
-        nc.gpsimd.memset(cs_all[:].bitcast(I32), 0)
+        ks_late = pool.tile([P, SLOTS], U8, name="ks_late", align_bytes=64)
+        nc.vector.memset(ks_all[:, : T // 2].bitcast(I32), 0)
+        nc.gpsimd.memset(ks_all[:, T // 2 :].bitcast(I32), 0)
+        nc.vector.memset(cs_all[:].bitcast(I32), 0)
+        nc.gpsimd.memset(ks_late[:].bitcast(I32), 0)
 
         nc.sync.dma_start(offsets[:], offs)
-        load_words(kw_all, k_words[0])
-        load_q(0)
-        load_q(1)
-        cw_all = [pool.tile([P, T], U32, name="cw_all0")]
-        load_words(cw_all[0], c_words[0])
-        for Q in range(QUADRANTS):
-            nc.scalar.dma_start(
-                out=ks_all[32 * Q : 32 * Q + 4, :].bitcast(I32).rearrange("f (g t) -> f g t", g=PASSES),
-                in_=k_scales[:, 4 * Q : 4 * Q + 4, :].bitcast(I32).rearrange("g f t -> f g t"),
+        for t0 in range(0, 3 * T // 4, T // 4):
+            load_words(kw_all[:, t0 : t0 + T // 4], k_words[0, :, t0 : t0 + T // 4, :])
+        for j in range(4):
+            nc.sync.dma_start(
+                out=ks_all[j:P:16, :].bitcast(I32),
+                in_=k_scales[:, j:16:4, :].bitcast(I32).rearrange("g q t -> q g t"),
             )
+        load_words(kw_all[:, 3 * T // 4 :], k_words[0, :, 3 * T // 4 :, :])
+        load_q(0)
         for Q in range(QUADRANTS):
-            nc.gpsimd.dma_start(
+            nc.sync.dma_start(
                 out=cs_all[32 * Q + 4 : 32 * Q + 12, :].bitcast(I32),
                 in_=c_scales[:, 4 * Q : 4 * Q + 4, :].bitcast(I32),
             )
+        load_q(1)
 
         q_bf = [pool.tile([P, NQ, PACK], BF16, name=f"q_bf{g}", tag=f"scratch{g}", align_bytes=64) for g in range(PASSES)]
         q_codes = [pool.tile([P, NQ], U32, name=f"q_codes{g}", align_bytes=64) for g in range(PASSES)]
         q_scales = [pool.tile([P, NQ], U8, name=f"q_scales{g}", align_bytes=64) for g in range(PASSES)]
 
-        def interleave(dst, src):
-            nc.scalar.copy(
+        def interleave(copy, dst, src):
+            copy(
                 out=dst.rearrange("p (c i) t -> p c t i", i=4),
                 in_=src.rearrange("p t (c i) -> p c t i", i=4),
             )
@@ -81,25 +89,24 @@ def tile_attend_plh_mixglu_topk_kernel(tc, qT, k_words, k_scales, c_words, c_sca
 
         kw_listed = pool.tile([P, SLOTS], U32, name="kw_listed")
         kw = pool.tile([P, PASSES * SLOTS * 2], U8, name="kw", align_bytes=64)
+        ks = pool.tile([P, SLOTS], U8, name="ks", align_bytes=64)
+        cs = pool.tile([P, SLOTS], U8, name="cs", align_bytes=64)
+        nc.vector.tensor_copy(dealt(ks[:]), ks_all[:].indirect(offsets[:]))
         nc.vector.tensor_copy(kw_listed[:], kw_all[:].indirect(offsets[:]))
-        interleave(q_bf[0][:], q_raw[0][:])
-        cw_all.append(pool.tile([P, T], U32, name="cw_all1", tag="window"))
-        load_words(cw_all[1], c_words[1])
-
-        ks_listed = pool.tile([P, PASSES * SLOTS], U8, name="ks_listed")
-        ks = pool.tile([P, PASSES * SLOTS], U8, name="ks", align_bytes=64)
-        for g in range(PASSES):
-            nc.vector.tensor_copy(
-                ks_listed[:, g * SLOTS : (g + 1) * SLOTS], ks_all[:, g * T : (g + 1) * T].indirect(offsets[:])
+        for Q in range(QUADRANTS):
+            nc.sync.dma_start(
+                out=ks_late[32 * Q : 32 * Q + 4, :].bitcast(I32),
+                in_=ks[32 * Q + 16 : 32 * Q + 20, :].bitcast(I32),
             )
+        cw_all = pool.tile([P, PASSES * T], U32, name="cw_all", tag="window")
+        for g in range(PASSES):
+            load_words(cw_all[:, g * T : (g + 1) * T], c_words[g])
         nc.vector.tensor_copy(
             out=kw[:].bitcast(U16).rearrange("p (g r c i) -> p g c r i", g=PASSES, r=PACK, i=4),
             in_=kw_listed[:].bitcast(U16).rearrange("p (c i r g) -> p g c r i", g=PASSES, r=PACK, i=4),
         )
-        nc.vector.tensor_copy(
-            out=ks[:].rearrange("p (g r c i) -> p g c r i", g=PASSES, r=PACK, i=16),
-            in_=ks_listed[:].rearrange("p (g c i r) -> p g c r i", g=PASSES, r=PACK, i=16),
-        )
+        interleave(nc.scalar.copy, q_bf[0][:], q_raw[0][:])
+        nc.vector.tensor_copy(dealt(cs[:]), cs_all[:].indirect(offsets[:]))
         quantize_q(0)
 
         gate = [psum.tile([P, NQ], F32, name=f"gate{r}") for r in range(PACK)]
@@ -110,7 +117,7 @@ def tile_attend_plh_mixglu_topk_kernel(tc, qT, k_words, k_scales, c_words, c_sca
                 nc.tensor.matmul_mx(
                     out=gate[r][:],
                     lhsT=kw[:, 2 * first : 2 * (first + P)].bitcast(FP4X4),
-                    lhsT_scale=ks[:, first : first + P],
+                    lhsT_scale=(ks, ks_late)[g][:, r * P : (r + 1) * P],
                     rhs=q_codes[g][:].bitcast(FP8X4),
                     rhs_scale=q_scales[g][:],
                     start=(g == 0),
@@ -118,14 +125,8 @@ def tile_attend_plh_mixglu_topk_kernel(tc, qT, k_words, k_scales, c_words, c_sca
                 )
 
         gate_pass(0)
-        interleave(q_bf[1][:], q_raw[1][:])
-        cs_listed = pool.tile([P, SLOTS], U8, name="cs_listed", tag="scratch0", align_bytes=64)
-        cs = pool.tile([P, SLOTS], U8, name="cs", align_bytes=64)
-        nc.vector.tensor_copy(cs_listed[:], cs_all[:].indirect(offsets[:]))
-        nc.vector.tensor_copy(
-            out=cs[:].rearrange("p (r c i) -> p c r i", r=PACK, i=16),
-            in_=cs_listed[:].rearrange("p (c i r) -> p c r i", r=PACK, i=16),
-        )
+        interleave(nc.scalar.copy, q_bf[1][:, :SPLIT, :], q_raw[1][:, :, :SPLIT])
+        interleave(nc.vector.tensor_copy, q_bf[1][:, SPLIT:, :], q_raw[1][:, :, SPLIT:])
         quantize_q(1)
         gate_pass(1)
 
@@ -134,21 +135,16 @@ def tile_attend_plh_mixglu_topk_kernel(tc, qT, k_words, k_scales, c_words, c_sca
             nc.scalar.activation(sig[:, r, :], gate[r][:], mybir.ActivationFunctionType.Sigmoid)
 
         layer = [psum.tile([P, PACK, CHUNK], F32, name=f"layer{j}") for j in range(CHUNKS)]
-        cw = [pool.tile([P, SLOTS], U32, name=f"cw{g}", align_bytes=64) for g in range(PASSES)]
+        cw = pool.tile([P, PASSES * SLOTS], U32, name="cw", tag="scratch1", align_bytes=64)
         for g in range(PASSES):
-            cw_listed = pool.tile([P, SLOTS], U32, name=f"cw_listed{g}", tag="scratch1", align_bytes=64)
-            nc.vector.tensor_copy(cw_listed[:], cw_all[g][:].indirect(offsets[:]))
-            nc.vector.tensor_copy(
-                out=cw[g][:].bitcast(I32).rearrange("p (r c i) -> p c r i", r=PACK, i=4),
-                in_=cw_listed[:].bitcast(I32).rearrange("p (c i r) -> p c r i", r=PACK, i=4),
-            )
+            nc.vector.tensor_copy(dealt(cw[:, g * SLOTS : (g + 1) * SLOTS]), cw_all[:, g * T : (g + 1) * T].indirect(offsets[:]))
             for j in range(CHUNKS):
                 cols = slice(j * CHUNK, (j + 1) * CHUNK)
                 for r in range(PACK):
                     slots = slice(r * P, (r + 1) * P)
                     nc.tensor.matmul_mx(
                         out=layer[j][:, r, :],
-                        lhsT=cw[g][:, slots].bitcast(FP8X4),
+                        lhsT=cw[:, g * SLOTS + r * P : g * SLOTS + (r + 1) * P].bitcast(FP8X4),
                         lhsT_scale=cs[4 * (g + 1) :, slots],
                         rhs=q_codes[g][:, cols].bitcast(FP8X4),
                         rhs_scale=q_scales[g][:, cols],
@@ -166,7 +162,7 @@ def tile_attend_plh_mixglu_topk_kernel(tc, qT, k_words, k_scales, c_words, c_sca
             cols = slice(j * CHUNK, (j + 1) * CHUNK)
             nc.vector.tensor_tensor(y[j][:], layer[j][:], sig[:, :, cols], mybir.AluOpType.mult)
             nc.sync.dma_start(out=y_rows[:, :, cols], in_=y[j][:])
-            interleave(y_bf[:, cols, :], y[j][:])
+            interleave(nc.scalar.copy, y_bf[:, cols, :], y[j][:])
         for cols in (slice(0, NQ - CHUNK), slice(NQ - CHUNK, NQ)):
             nc.vector.quantize_mx(
                 out=y_codes[:, cols].bitcast(FP8X4),

@@ -22,6 +22,7 @@ QUADRANTS = 4
 CHUNK = 128
 CHUNKS = NQ // CHUNK
 SPLIT = 320
+STRIP = 64
 
 
 def dealt(ap):
@@ -50,12 +51,12 @@ def tile_attend_plh_mixglu_topk_kernel(tc, qT, k_words, k_scales, c_words, c_sca
         ks_late = pool.tile([P, SLOTS], U8, name="ks_late", align_bytes=64)
         nc.vector.memset(ks_all[:, : T // 2].bitcast(I32), 0)
         nc.gpsimd.memset(ks_all[:, T // 2 :].bitcast(I32), 0)
-        nc.vector.memset(cs_all[:].bitcast(I32), 0)
-        nc.gpsimd.memset(ks_late[:].bitcast(I32), 0)
+        nc.gpsimd.memset(cs_all[:].bitcast(I32), 0)
+        nc.vector.memset(ks_late[:].bitcast(I32), 0)
 
         nc.sync.dma_start(offsets[:], offs)
-        for t0 in range(0, 3 * T // 4, T // 4):
-            load_words(kw_all[:, t0 : t0 + T // 4], k_words[0, :, t0 : t0 + T // 4, :])
+        for t0, t1 in ((0, 256), (256, 896), (896, 1536)):
+            load_words(kw_all[:, t0:t1], k_words[0, :, t0:t1, :])
         for j in range(4):
             nc.sync.dma_start(
                 out=ks_all[j:P:16, :].bitcast(I32),
@@ -64,7 +65,7 @@ def tile_attend_plh_mixglu_topk_kernel(tc, qT, k_words, k_scales, c_words, c_sca
         load_words(kw_all[:, 3 * T // 4 :], k_words[0, :, 3 * T // 4 :, :])
         load_q(0)
         for Q in range(QUADRANTS):
-            nc.sync.dma_start(
+            nc.gpsimd.dma_start(
                 out=cs_all[32 * Q + 4 : 32 * Q + 12, :].bitcast(I32),
                 in_=c_scales[:, 4 * Q : 4 * Q + 4, :].bitcast(I32),
             )
@@ -87,10 +88,9 @@ def tile_attend_plh_mixglu_topk_kernel(tc, qT, k_words, k_scales, c_words, c_sca
                 in_=q_bf[g][:].rearrange("p n t -> p (n t)"),
             )
 
-        kw_listed = pool.tile([P, SLOTS], U32, name="kw_listed")
+        kw_listed = pool.tile([P, SLOTS], U32, name="kw_listed", tag="listed", align_bytes=64)
         kw = pool.tile([P, PASSES * SLOTS * 2], U8, name="kw", align_bytes=64)
         ks = pool.tile([P, SLOTS], U8, name="ks", align_bytes=64)
-        cs = pool.tile([P, SLOTS], U8, name="cs", align_bytes=64)
         nc.vector.tensor_copy(dealt(ks[:]), ks_all[:].indirect(offsets[:]))
         nc.vector.tensor_copy(kw_listed[:], kw_all[:].indirect(offsets[:]))
         for Q in range(QUADRANTS):
@@ -106,6 +106,7 @@ def tile_attend_plh_mixglu_topk_kernel(tc, qT, k_words, k_scales, c_words, c_sca
             in_=kw_listed[:].bitcast(U16).rearrange("p (c i r g) -> p g c r i", g=PASSES, r=PACK, i=4),
         )
         interleave(nc.scalar.copy, q_bf[0][:], q_raw[0][:])
+        cs = pool.tile([P, SLOTS], U8, name="cs", tag="listed", align_bytes=64)
         nc.vector.tensor_copy(dealt(cs[:]), cs_all[:].indirect(offsets[:]))
         quantize_q(0)
 
@@ -159,10 +160,12 @@ def tile_attend_plh_mixglu_topk_kernel(tc, qT, k_words, k_scales, c_words, c_sca
         y = [pool.tile([P, PACK, CHUNK], F32, name=f"y{j}") for j in range(CHUNKS)]
         y_bf = pool.tile([P, NQ, PACK], BF16, name="y_bf", align_bytes=64)
         for j in range(CHUNKS):
-            cols = slice(j * CHUNK, (j + 1) * CHUNK)
-            nc.vector.tensor_tensor(y[j][:], layer[j][:], sig[:, :, cols], mybir.AluOpType.mult)
-            nc.sync.dma_start(out=y_rows[:, :, cols], in_=y[j][:])
-            interleave(nc.scalar.copy, y_bf[:, cols, :], y[j][:])
+            for n0 in range(0, CHUNK, STRIP):
+                part = slice(n0, n0 + STRIP)
+                cols = slice(j * CHUNK + n0, j * CHUNK + n0 + STRIP)
+                nc.vector.tensor_tensor(y[j][:, :, part], layer[j][:, :, part], sig[:, :, cols], mybir.AluOpType.mult)
+                interleave(nc.scalar.copy, y_bf[:, cols, :], y[j][:, :, part])
+            nc.sync.dma_start(out=y_rows[:, :, j * CHUNK : (j + 1) * CHUNK], in_=y[j][:])
         for cols in (slice(0, NQ - CHUNK), slice(NQ - CHUNK, NQ)):
             nc.vector.quantize_mx(
                 out=y_codes[:, cols].bitcast(FP8X4),

@@ -36,7 +36,7 @@ def tile_attend_plh_mixglu_topk_kernel(tc, qT, k_words, k_scales, c_words, c_sca
         psum = ctx.enter_context(tc.psum_pool(name="psum", bufs=1))
 
         offsets = pool.tile([P, SLOTS // 16], U16, name="offsets")
-        q_raw = [pool.tile([P, PACK, NQ], F32, name=f"q_raw{g}") for g in range(PASSES)]
+        q_raw = [pool.tile([P, PACK, NQ], F32, name=f"q_raw{g}", tag=f"raw{g}", align_bytes=64) for g in range(PASSES)]
         kw_all = pool.tile([P, T], U32, name="kw_all")
         ks_all = pool.tile([P, T], U8, name="ks_all", tag="window")
         cs_all = pool.tile([P, T], U8, name="cs_all")
@@ -88,7 +88,7 @@ def tile_attend_plh_mixglu_topk_kernel(tc, qT, k_words, k_scales, c_words, c_sca
                 in_=q_bf[g][:].rearrange("p n t -> p (n t)"),
             )
 
-        kw_listed = pool.tile([P, SLOTS], U32, name="kw_listed", tag="listed", align_bytes=64)
+        kw_listed = pool.tile([P, SLOTS], U32, name="kw_listed")
         kw = pool.tile([P, PASSES * SLOTS * 2], U8, name="kw", align_bytes=64)
         ks = pool.tile([P, SLOTS], U8, name="ks", align_bytes=64)
         nc.vector.tensor_copy(dealt(ks[:]), ks_all[:].indirect(offsets[:]))
@@ -106,8 +106,6 @@ def tile_attend_plh_mixglu_topk_kernel(tc, qT, k_words, k_scales, c_words, c_sca
             in_=kw_listed[:].bitcast(U16).rearrange("p (c i r g) -> p g c r i", g=PASSES, r=PACK, i=4),
         )
         interleave(nc.scalar.copy, q_bf[0][:], q_raw[0][:])
-        cs = pool.tile([P, SLOTS], U8, name="cs", tag="listed", align_bytes=64)
-        nc.vector.tensor_copy(dealt(cs[:]), cs_all[:].indirect(offsets[:]))
         quantize_q(0)
 
         gate = [psum.tile([P, NQ], F32, name=f"gate{r}") for r in range(PACK)]
@@ -129,6 +127,8 @@ def tile_attend_plh_mixglu_topk_kernel(tc, qT, k_words, k_scales, c_words, c_sca
         interleave(nc.scalar.copy, q_bf[1][:, :SPLIT, :], q_raw[1][:, :, :SPLIT])
         interleave(nc.vector.tensor_copy, q_bf[1][:, SPLIT:, :], q_raw[1][:, :, SPLIT:])
         quantize_q(1)
+        cs = pool.tile([P, SLOTS], U8, name="cs", tag="raw1", align_bytes=64)
+        nc.vector.tensor_copy(dealt(cs[:]), cs_all[:].indirect(offsets[:]))
         gate_pass(1)
 
         sig = pool.tile([P, PACK, NQ], F32, name="sig")

from contextlib import ExitStack

import concourse.mybir as mybir

D, T, SLOTS, NQ = 1024, 2048, 512, 512
FLOPS = 2 * 2 * SLOTS * NQ * D

F32 = mybir.dt.float32
BF16 = mybir.dt.bfloat16
I32 = mybir.dt.int32
U32 = mybir.dt.uint32
U16 = mybir.dt.uint16
U8 = mybir.dt.uint8
FP8X4 = mybir.dt.float8_e4m3fn_x4
FP4X4 = mybir.dt.float4_e2m1fn_x4

P = 128
PACK = 4
K_PASS = P * PACK
PASSES = D // K_PASS
QUADRANTS = 4
CHUNK = 128
CHUNKS = NQ // CHUNK
SPLIT = 320
STRIP = 64


def dealt(ap):
    return ap.rearrange("p (r s) -> p s r", r=PACK)


def tile_attend_plh_mixglu_topk_kernel(tc, qT, k_words, k_scales, c_words, c_scales, offs, out_0, out_1, out_2):
    nc = tc.nc
    with ExitStack() as ctx:
        pool = ctx.enter_context(tc.tile_pool(name="held", bufs=1))
        psum = ctx.enter_context(tc.psum_pool(name="psum", bufs=1))

        offsets = pool.tile([P, SLOTS // 16], U16, name="offsets")
        q_raw = [pool.tile([P, PACK, NQ], F32, name=f"q_raw{g}", tag=f"raw{g}", align_bytes=64) for g in range(PASSES)]
        kw_all = pool.tile([P, T], U32, name="kw_all")
        ks_all = pool.tile([P, T], U8, name="ks_all", tag="window")
        cs_all = pool.tile([P, T], U8, name="cs_all")

        def load_q(g):
            rows = qT[0, g * K_PASS : (g + 1) * K_PASS, :]
            nc.sync.dma_start(out=q_raw[g][:], in_=rows.rearrange("(p j) n -> p j n", j=PACK))

        def load_words(tile, words):
            nc.sync.dma_start(out=tile.bitcast(I32), in_=words.rearrange("p t b -> p (t b)").bitcast(I32))

        ks_late = pool.tile([P, SLOTS], U8, name="ks_late", align_bytes=64)
        nc.vector.memset(ks_all[:, : T // 2].bitcast(I32), 0)
        nc.gpsimd.memset(ks_all[:, T // 2 :].bitcast(I32), 0)
        nc.gpsimd.memset(cs_all[:].bitcast(I32), 0)
        nc.vector.memset(ks_late[:].bitcast(I32), 0)

        nc.sync.dma_start(offsets[:], offs)
        for t0, t1 in ((0, 256), (256, 896), (896, 1536)):
            load_words(kw_all[:, t0:t1], k_words[0, :, t0:t1, :])
        for j in range(4):
            nc.sync.dma_start(
                out=ks_all[j:P:16, :].bitcast(I32),
                in_=k_scales[:, j:16:4, :].bitcast(I32).rearrange("g q t -> q g t"),
            )
        load_words(kw_all[:, 3 * T // 4 :], k_words[0, :, 3 * T // 4 :, :])
        load_q(0)
        for Q in range(QUADRANTS):
            nc.gpsimd.dma_start(
                out=cs_all[32 * Q + 4 : 32 * Q + 12, :].bitcast(I32),
                in_=c_scales[:, 4 * Q : 4 * Q + 4, :].bitcast(I32),
            )
        load_q(1)

        q_bf = [pool.tile([P, NQ, PACK], BF16, name=f"q_bf{g}", tag=f"scratch{g}", align_bytes=64) for g in range(PASSES)]
        q_codes = [pool.tile([P, NQ], U32, name=f"q_codes{g}", align_bytes=64) for g in range(PASSES)]
        q_scales = [pool.tile([P, NQ], U8, name=f"q_scales{g}", align_bytes=64) for g in range(PASSES)]

        def interleave(copy, dst, src):
            copy(
                out=dst.rearrange("p (c i) t -> p c t i", i=4),
                in_=src.rearrange("p t (c i) -> p c t i", i=4),
            )

        def quantize_q(g):
            nc.vector.quantize_mx(
                out=q_codes[g][:].bitcast(FP8X4),
                scales=q_scales[g][:],
                in_=q_bf[g][:].rearrange("p n t -> p (n t)"),
            )

        kw_listed = pool.tile([P, SLOTS], U32, name="kw_listed")
        kw = pool.tile([P, PASSES * SLOTS * 2], U8, name="kw", align_bytes=64)
        ks = pool.tile([P, SLOTS], U8, name="ks", align_bytes=64)
        nc.vector.tensor_copy(dealt(ks[:]), ks_all[:].indirect(offsets[:]))
        nc.vector.tensor_copy(kw_listed[:], kw_all[:].indirect(offsets[:]))
        for Q in range(QUADRANTS):
            nc.sync.dma_start(
                out=ks_late[32 * Q : 32 * Q + 4, :].bitcast(I32),
                in_=ks[32 * Q + 16 : 32 * Q + 20, :].bitcast(I32),
            )
        cw_all = pool.tile([P, PASSES * T], U32, name="cw_all", tag="window")
        for g in range(PASSES):
            load_words(cw_all[:, g * T : (g + 1) * T], c_words[g])
        nc.vector.tensor_copy(
            out=kw[:].bitcast(U16).rearrange("p (g r c i) -> p g c r i", g=PASSES, r=PACK, i=4),
            in_=kw_listed[:].bitcast(U16).rearrange("p (c i r g) -> p g c r i", g=PASSES, r=PACK, i=4),
        )
        interleave(nc.scalar.copy, q_bf[0][:], q_raw[0][:])
        quantize_q(0)

        gate = [psum.tile([P, NQ], F32, name=f"gate{r}") for r in range(PACK)]

        def gate_pass(g):
            for r in range(PACK):
                first = g * SLOTS + r * P
                nc.tensor.matmul_mx(
                    out=gate[r][:],
                    lhsT=kw[:, 2 * first : 2 * (first + P)].bitcast(FP4X4),
                    lhsT_scale=(ks, ks_late)[g][:, r * P : (r + 1) * P],
                    rhs=q_codes[g][:].bitcast(FP8X4),
                    rhs_scale=q_scales[g][:],
                    start=(g == 0),
                    stop=(g == PASSES - 1),
                )

        gate_pass(0)
        interleave(nc.scalar.copy, q_bf[1][:, :SPLIT, :], q_raw[1][:, :, :SPLIT])
        interleave(nc.vector.tensor_copy, q_bf[1][:, SPLIT:, :], q_raw[1][:, :, SPLIT:])
        quantize_q(1)
        cs = pool.tile([P, SLOTS], U8, name="cs", tag="raw1", align_bytes=64)
        nc.vector.tensor_copy(dealt(cs[:]), cs_all[:].indirect(offsets[:]))
        gate_pass(1)

        sig = pool.tile([P, PACK, NQ], F32, name="sig")
        for r in range(PACK):
            nc.scalar.activation(sig[:, r, :], gate[r][:], mybir.ActivationFunctionType.Sigmoid)

        layer = [psum.tile([P, PACK, CHUNK], F32, name=f"layer{j}") for j in range(CHUNKS)]
        cw = pool.tile([P, PASSES * SLOTS], U32, name="cw", tag="scratch1", align_bytes=64)
        for g in range(PASSES):
            nc.vector.tensor_copy(dealt(cw[:, g * SLOTS : (g + 1) * SLOTS]), cw_all[:, g * T : (g + 1) * T].indirect(offsets[:]))
            for j in range(CHUNKS):
                cols = slice(j * CHUNK, (j + 1) * CHUNK)
                for r in range(PACK):
                    slots = slice(r * P, (r + 1) * P)
                    nc.tensor.matmul_mx(
                        out=layer[j][:, r, :],
                        lhsT=cw[:, g * SLOTS + r * P : g * SLOTS + (r + 1) * P].bitcast(FP8X4),
                        lhsT_scale=cs[4 * (g + 1) :, slots],
                        rhs=q_codes[g][:, cols].bitcast(FP8X4),
                        rhs_scale=q_scales[g][:, cols],
                        start=(g == 0 and r == 0),
                        stop=(g == PASSES - 1 and r == PACK - 1),
                    )

        y_codes = pool.tile([P, NQ], U32, name="y_codes", align_bytes=64)
        y_scales = pool.tile([P, NQ], U8, name="y_scales", align_bytes=64)
        y_rows = out_0.rearrange("(p r) n -> p r n", r=PACK)
        code_rows = out_1[0].rearrange("p n u -> p (n u)").bitcast(I32)
        y = [pool.tile([P, PACK, CHUNK], F32, name=f"y{j}") for j in range(CHUNKS)]
        y_bf = pool.tile([P, NQ, PACK], BF16, name="y_bf", align_bytes=64)
        for j in range(CHUNKS):
            for n0 in range(0, CHUNK, STRIP):
                part = slice(n0, n0 + STRIP)
                cols = slice(j * CHUNK + n0, j * CHUNK + n0 + STRIP)
                nc.vector.tensor_tensor(y[j][:, :, part], layer[j][:, :, part], sig[:, :, cols], mybir.AluOpType.mult)
                interleave(nc.scalar.copy, y_bf[:, cols, :], y[j][:, :, part])
            nc.sync.dma_start(out=y_rows[:, :, j * CHUNK : (j + 1) * CHUNK], in_=y[j][:])
        for cols in (slice(0, NQ - CHUNK), slice(NQ - CHUNK, NQ)):
            nc.vector.quantize_mx(
                out=y_codes[:, cols].bitcast(FP8X4),
                scales=y_scales[:, cols],
                in_=y_bf[:, cols, :].rearrange("p n t -> p (n t)"),
            )
            nc.scalar.dma_start(out=code_rows[:, cols], in_=y_codes[:, cols].bitcast(I32))
        for Q in range(QUADRANTS):
            queue = nc.sync if Q % 2 == 0 else nc.scalar
            queue.dma_start(
                out=out_2[0, 4 * Q : 4 * Q + 4, :].bitcast(I32),
                in_=y_scales[32 * Q : 32 * Q + 4, :].bitcast(I32),
            )
